import numpy as np
import ml_dtypes


def mxq(x, axis, fmt="e4m3"):
    dtype, down = {"e4m3": (ml_dtypes.float8_e4m3fn, 7), "e5m2": (ml_dtypes.float8_e5m2, 14)}[fmt]
    v = np.moveaxis(np.asarray(x, np.float32).astype(ml_dtypes.bfloat16).astype(np.float64), axis, -1)
    blocks = v.reshape(v.shape[:-1] + (-1, 32))
    amax = np.abs(blocks).max(-1, keepdims=True)
    byte = np.maximum(np.where(amax > 0, np.frexp(amax)[1] - 1 + 127, 0) - down, 1)
    scale = np.exp2(byte - 127.0)
    codes = (blocks / scale).astype(np.float32).astype(dtype).astype(np.float64)
    return np.moveaxis((codes * scale).reshape(v.shape), -1, axis)


WIDE = False


def mx_kscale(k):
    if not WIDE:
        return np.ones(k)
    levels = np.array([10, -10, 5, -5, 0])
    if k % 512:
        return np.exp2(np.random.permutation(np.resize(levels, k // 32))).repeat(32)
    a = np.empty((k // 512, 16))
    for p in range(k // 512):
        a[p, :8] = np.random.permutation(np.resize(levels, 8))
        for g in range(8):
            far = levels[np.abs(levels - a[p, g]) >= 10]
            a[p, g + 8] = far[np.random.randint(len(far))]
    return np.exp2(a.ravel()).repeat(32)


def f64(x):
    return np.asarray(x).astype(np.float64)


def striped(idx):
    return np.tile(idx.reshape(-1, 16).T, (8, 1)).astype(np.uint16)


def unstriped(offs):
    return offs[:16].T.reshape(-1).astype(np.int64)


E2M1 = np.array([0.0, 0.5, 1.0, 1.5, 2.0, 3.0, 4.0, 6.0, -0.0, -0.5, -1.0, -1.5, -2.0, -3.0, -4.0, -6.0])


def pack_weight(w, fmt):
    k, n = w.shape
    w = f64(np.asarray(w, np.float32).astype(ml_dtypes.bfloat16)).reshape(k // 32, 32, n)
    amax = np.abs(w).max(1)
    if fmt == "e4m3":
        byte = np.frexp(amax)[1] - 1 + 127 - 7
    else:
        mant, ex = np.frexp(amax / 6.0)
        byte = np.where(mant > 0.5, ex, ex - 1) + 127
    byte = np.clip(np.where(amax > 0, byte, 1), 1, 254)
    scaled = (w * np.exp2(127.0 - byte)[:, None, :]).reshape(k, n).astype(np.float32)
    by_word = np.ascontiguousarray(scaled.reshape(k // 512, 128, 4, n).transpose(0, 1, 3, 2))
    if fmt == "e4m3":
        words = by_word.astype(ml_dtypes.float8_e4m3fn).view(np.uint8)
    else:
        c = by_word.astype(ml_dtypes.float4_e2m1fn).view(np.uint8) & 0xF
        words = (c[..., 0::2] | (c[..., 1::2] << 4)).reshape(k // 512, 128, 2 * n)
    return np.ascontiguousarray(words), np.ascontiguousarray(byte.astype(np.uint8).reshape(k // 512, 16, n))


def unpack_weight(words, scales, fmt):
    g, _, n = scales.shape
    words = np.ascontiguousarray(words).reshape(g, 128, n, -1)
    if fmt == "e4m3":
        vals = words.view(ml_dtypes.float8_e4m3fn).astype(np.float64)
    else:
        nib = np.empty((g, 128, n, 4), np.uint8)
        nib[..., 0::2] = words & 0xF
        nib[..., 1::2] = words >> 4
        vals = E2M1[nib]
    vals = vals * np.repeat(np.exp2(scales.astype(np.float64) - 127.0), 8, axis=1)[..., None]
    return vals.transpose(0, 1, 3, 2).reshape(g * 512, n)


def gelu(v):
    return 0.5 * v * (1.0 + np.tanh(np.sqrt(2.0 / np.pi) * (v + 0.044715 * v**3)))


def bf(x):
    return np.asarray(x, np.float32).astype(ml_dtypes.bfloat16)


def planes(Y):
    n, m = Y.shape
    b = f64(bf(Y)).reshape(n // 32, 32, m)
    amax = np.abs(b).max(1)
    byte = np.clip(np.where(amax > 0, np.frexp(amax)[1] - 1 + 127 - 7, 1), 1, 254)
    codes = (b * np.exp2(127.0 - byte)[:, None, :]).reshape(n, m).astype(np.float32).astype(ml_dtypes.float8_e4m3fn).view(np.uint8)
    words = codes.reshape(n // 512, 128, 4, m).transpose(0, 1, 3, 2)
    return np.ascontiguousarray(words), np.ascontiguousarray(byte.astype(np.uint8).reshape(n // 512, 16, m))


K, H, N, T, S, T2, P = 1024, 1024, 512, 2048, 1024, 2048, 512


def setup_inputs():
    n = np.random.standard_normal
    s = mx_kscale(K)[:, None]
    u = mx_kscale(H)[:, None]
    spread = np.exp(0.8 * n(N))[None, :]
    tab_words, tab_scales = pack_weight(n((K, T)) * s, "e4m3")
    w4_words, w4_scales = pack_weight(n((H, N)) / np.sqrt(H) * spread / u, "e2m1")
    return {
        "tab_words": tab_words, "tab_scales": tab_scales,
        "offs": striped(np.random.permutation(T)[:S]),
        "offs2": striped(np.random.permutation(T2)[:S]),
        "offs3": striped(np.random.permutation(T2)[:P]),
        "w1": (0.7 * n((K, H)) / np.sqrt(K) / s).astype(np.float32),
        "duty": np.random.uniform(0.5, 1.5, S).astype(np.float32),
        "wgs": np.exp(0.3 * n((128, S))).astype(np.float32),
        "page0": (0.8 * n((H, T2))).astype(np.float32),
        "steep": np.random.uniform(1, 3, H).astype(np.float32),
        "share": np.random.uniform(0.1, 0.5, H).astype(np.float32),
        "wear": (2.0 * n((H, P)) * u).astype(np.float32),
        "gain": (np.random.uniform(1, 3, H) * np.sign(n(H)) * u[:, 0]).astype(np.float32),
        "w4_words": w4_words, "w4_scales": w4_scales,
        "w5": (n((H, N)) / np.sqrt(H) * spread / u).astype(np.float32),
    }


def reference(tab_words, tab_scales, offs, offs2, offs3, w1, duty, wgs, page0,
              steep, share, wear, gain, w4_words, w4_scales, w5):
    v = unpack_weight(tab_words, tab_scales, "e4m3")[:, unstriped(offs)]
    h = (mxq(f64(w1), 0, "e4m3").T @ v) * f64(duty)[None, :]
    page = f64(page0).copy()
    page[:, unstriped(offs2)] = np.tile(f64(wgs), (H // 128, 1)) * h
    top = page.max(axis=1)
    a = 1.0 / (1.0 + np.exp(-f64(steep)[:, None] * (page[:, unstriped(offs3)] - f64(share)[:, None] * top[:, None])))
    x1 = mxq(a * f64(wear), 0, "e4m3")
    x2 = mxq(a * f64(gain)[:, None], 0, "e4m3")
    w4 = unpack_weight(w4_words, w4_scales, "e2m1")
    y = w4.T @ x1 + mxq(f64(w5), 0, "e4m3").T @ x2
    words, scales = planes(y)
    return y, words, scales

@@ -1,0 +1,356 @@
+from contextlib import ExitStack
+
+import concourse.mybir as mybir
+from concourse.masks import make_identity
+
+K, H, N, T, S, T2, LOOK = 1024, 1024, 512, 2048, 1024, 2048, 512
+FLOPS = 2 * K * H * S + 2 * 2 * H * N * LOOK
+
+F32 = mybir.dt.float32
+BF16 = mybir.dt.bfloat16
+I32 = mybir.dt.int32
+U32 = mybir.dt.uint32
+U16 = mybir.dt.uint16
+U8 = mybir.dt.uint8
+FP8X4 = mybir.dt.float8_e4m3fn_x4
+FP4X4 = mybir.dt.float4_e2m1fn_x4
+ALU = mybir.AluOpType
+ACT = mybir.ActivationFunctionType
+AXIS = mybir.AxisListType
+
+P = 128
+PACK = 4
+PASS = P * PACK
+BANK = 512
+QUARTER = 128
+
+
+def tile_list_jetbridge_fault_scores_kernel(
+    tc, tab_words, tab_scales, offs, offs2, offs3, w1, duty, wgs, page0, steep, share, wear, gain,
+    w4_words, w4_scales, w5, out_0, out_1, out_2,
+):
+    nc = tc.nc
+    with ExitStack() as ctx:
+        lists = ctx.enter_context(tc.tile_pool(name="lists", bufs=1))
+        sb = ctx.enter_context(tc.tile_pool(name="sb", bufs=1))
+        psum = ctx.enter_context(tc.psum_pool(name="psum", bufs=1))
+
+        def sbuf(shape, dtype, name, tag=None, bufs=1):
+            return sb.tile(shape, dtype, name=name, tag=tag or name, bufs=bufs, align_bytes=64)
+
+        pick = lists.tile([P, S // 16], U16, name="pick")
+        place = lists.tile([P, S // 16], U16, name="place")
+        look = lists.tile([P, LOOK // 16], U16, name="look")
+        nc.sync.dma_start(pick[:], offs)
+
+        tab_sc = sbuf([P, T], U8, "tab_sc")
+        nc.vector.memset(tab_sc[:].bitcast(I32), 0)
+        for q in range(4):
+            nc.sync.dma_start(out=tab_sc[32 * q : 32 * q + 8, :].bitcast(I32), in_=tab_scales[:, 4 * q : 4 * q + 4, :].bitcast(I32))
+        tab_w = [sbuf([P, T], I32, f"tab_w{a}") for a in range(2)]
+
+        def load_tab(a):
+            nc.sync.dma_start(out=tab_w[a][:], in_=tab_words[a].rearrange("p t i -> p (t i)").bitcast(I32))
+
+        def k_rows(w, a, c0, c1):
+            return w[PASS * a : PASS * (a + 1), c0:c1].rearrange("(p j) c -> p j c", j=PACK)
+
+        load_tab(0)
+        w1_nat = {}
+
+        def load_w1_nat(u):
+            for a in range(2):
+                w1_nat[u, a] = sbuf([P, PACK, 256], F32, f"w1_nat{u}{a}", tag="raw4", bufs=4)
+                nc.sync.dma_start(out=w1_nat[u, a][:], in_=k_rows(w1, a, 256 * u, 256 * (u + 1)))
+
+        load_w1_nat(0)
+        load_tab(1)
+        duty_col = sbuf([P, 2, PACK], F32, "duty_col")
+        nc.sync.dma_start(out=duty_col[:], in_=duty.rearrange("(h p c) -> p h c", h=2, c=PACK))
+        wd_nat = sbuf([P, S], F32, "wd_nat")
+        nc.sync.dma_start(out=wd_nat[:], in_=wgs)
+        nc.sync.dma_start(place[:], offs2)
+
+        pages = {}
+
+        def load_page(s):
+            pages[s] = sbuf([P, T2], F32, f"page{s}", tag="page", bufs=6)
+            if s < 4:
+                rows = page0[P * s : P * (s + 1), :]
+            else:
+                rows = page0[PASS:, :].rearrange("(p t) c -> p t c", t=PACK)[:, s - 4, :]
+            nc.sync.dma_start(out=pages[s][:], in_=rows)
+
+        load_page(0)
+        load_w1_nat(1)
+
+        got_sc = sbuf([P, S], U8, "got_sc")
+        nc.vector.tensor_copy(got_sc[:], tab_sc[:].indirect(pick[:]))
+        got_w = {}
+
+        def gather_words(a):
+            for h in range(2):
+                got_w[a, h] = sbuf([P, BANK], U32, f"got_w{a}{h}")
+                nc.vector.tensor_copy(got_w[a, h][:], tab_w[a][:].bitcast(U32).indirect(pick[:, 32 * h : 32 * (h + 1)]))
+
+        gather_words(0)
+
+        w1_codes = {}
+        w1_sc = {}
+
+        def quantise_w1_nat(s):
+            grouped = sbuf([P, 2, P, PACK], BF16, f"w1_bf{s}", tag="w1_bf", bufs=2)
+            for a in range(2):
+                raw = w1_nat[s // 2, a][:, :, P * (s % 2) : P * (s % 2 + 1)]
+                nc.scalar.copy(out=grouped[:, a].rearrange("p (c i) j -> p c j i", i=4), in_=raw.rearrange("p j (c i) -> p c j i", i=4))
+            codes = sbuf([P, 2 * P], U32, f"w1_codes{s}")
+            scales = sbuf([P, 2 * P], U8, f"w1_sc{s}")
+            nc.vector.quantize_mx(out=codes[:].bitcast(FP8X4), scales=scales[:], in_=grouped[:].rearrange("p a c j -> p (a c j)"))
+            for a in range(2):
+                w1_codes[s, a] = codes[:, P * a : P * (a + 1)]
+                w1_sc[s, a] = scales[:, P * a : P * (a + 1)]
+
+        def quantise_dealt(raw, name):
+            grouped = sbuf([P, PACK, P, PACK], BF16, name + "_bf", tag="dealt_bf", bufs=2)
+            nc.scalar.copy(out=grouped[:].rearrange("p t m j -> p m j t"), in_=raw[:].rearrange("p j (m t) -> p m j t", t=PACK))
+            codes = sbuf([P, PASS], U32, name + "_codes")
+            scales = sbuf([P, PASS], U8, name + "_sc")
+            nc.vector.quantize_mx(out=codes[:].bitcast(FP8X4), scales=scales[:], in_=grouped[:].rearrange("p t m j -> p (t m j)"))
+            return codes, scales
+
+        quantise_w1_nat(0)
+        gather_words(1)
+
+        ident = sbuf([P, P], F32, "ident")
+        make_identity(nc, ident[:])
+        for h in range(2):
+            spread = psum.tile([P, PACK, P], F32, name=f"duty_ps{h}", tag="h", bufs=4)
+            for c in range(PACK):
+                nc.tensor.transpose(spread[:, c, :], duty_col[:, h, c : c + 1].to_broadcast([P, P]), ident[:])
+            cols = wd_nat[:, BANK * h : BANK * (h + 1)].rearrange("p (n c) -> p n c", c=PACK)
+            nc.vector.tensor_tensor(cols, spread[:].rearrange("p c n -> p n c"), cols, ALU.mult)
+
+        quantise_w1_nat(1)
+
+        sums = {}
+
+        def first_product(s):
+            sums[s] = sbuf([P, S], F32, f"sums{s}", tag="sums", bufs=3)
+            for h in range(2):
+                bank = psum.tile([P, BANK], F32, name=f"h_ps{s}{h}", tag="h", bufs=4)
+                for a in range(2):
+                    nc.tensor.matmul_mx(
+                        out=bank[:], lhsT=w1_codes[s, a].bitcast(FP8X4), lhsT_scale=w1_sc[s, a],
+                        rhs=got_w[a, h][:].bitcast(FP8X4), rhs_scale=got_sc[4 * a :, BANK * h : BANK * (h + 1)],
+                        start=(a == 0), stop=(a == 1),
+                    )
+                nc.scalar.copy(out=sums[s][:, BANK * h : BANK * (h + 1)], in_=bank[:])
+
+        first_product(0)
+        first_product(1)
+
+        nc.sync.dma_start(look[:], offs3)
+        steep_sb, share_sb = [], []
+        for name, vec, dst in (("steep", steep, steep_sb), ("share", share, share_sb)):
+            nat = sbuf([P, PACK], F32, name + "_nat")
+            with nc.allow_non_contiguous_dma(reason="one value of a row vector for each partition"):
+                nc.sync.dma_start(out=nat[:], in_=vec[:PASS].rearrange("(s p) -> p s", p=P))
+            dealt = sbuf([P, PACK], F32, name + "_dealt")
+            nc.sync.dma_start(out=dealt[:], in_=vec[PASS:].rearrange("(p t) -> p t", t=PACK))
+            dst.extend([nat, dealt])
+        gain_sb = sbuf([P, 2, PACK], F32, "gain_sb")
+        nc.sync.dma_start(out=gain_sb[:], in_=gain.rearrange("(b p t) -> p b t", b=2, t=PACK))
+        load_page(1)
+        w1_raw = []
+        for a in range(2):
+            raw = sbuf([P, PACK, PASS], F32, f"w1_raw{a}", tag="raw8", bufs=4)
+            nc.sync.dma_start(out=raw[:], in_=k_rows(w1, a, PASS, H))
+            w1_raw.append(raw)
+        load_page(2)
+
+        quantise_w1_nat(2)
+        quantise_w1_nat(3)
+
+        wd_dealt = []
+        for t in range(PACK):
+            dealt = sbuf([P, S], F32, f"wd_dealt{t}", tag="raw4", bufs=4)
+            for g in range(4):
+                nc.sync.dma_start(out=dealt[32 * g : 32 * (g + 1), :], in_=wd_nat[t:P:PACK, :])
+            wd_dealt.append(dealt)
+        load_page(3)
+
+        w5_raw, wear_sb = [], []
+
+        def load_second_stage(b):
+            raw = sbuf([P, PACK, N], F32, f"w5_raw{b}", tag="raw8", bufs=4)
+            nc.sync.dma_start(out=raw[:], in_=k_rows(w5, b, 0, N))
+            w5_raw.append(raw)
+            rows = sbuf([P, PACK, LOOK], F32, f"wear{b}", tag="raw8", bufs=4)
+            nc.sync.dma_start(out=rows[:], in_=k_rows(wear, b, 0, LOOK))
+            wear_sb.append(rows)
+
+        load_second_stage(0)
+        load_page(4)
+        load_page(5)
+        w4_raw = sbuf([P, 2, 2 * N], U8, "w4_raw")
+        nc.sync.dma_start(out=w4_raw[:].bitcast(I32), in_=w4_words.rearrange("a p c -> p a c").bitcast(I32))
+        w4_sc_raw = sbuf([P, 2, N], U8, "w4_sc_raw")
+        nc.gpsimd.memset(w4_sc_raw[:].bitcast(I32), 0)
+        for q in range(4):
+            nc.sync.dma_start(
+                out=w4_sc_raw[32 * q : 32 * q + 4].bitcast(I32),
+                in_=w4_scales[:, 4 * q : 4 * q + 4, :].rearrange("a r c -> r a c").bitcast(I32),
+            )
+
+        slope = []
+        for b in range(2):
+            neg = sbuf([P, PACK], F32, f"slope{b}")
+            nc.vector.scalar_tensor_tensor(neg[:], steep_sb[b][:], -1.0, share_sb[b][:], ALU.mult, ALU.mult)
+            slope.append(neg)
+
+        opened = [sbuf([P, PACK, LOOK], F32, f"opened{b}") for b in range(2)]
+        x1_bf = [sbuf([P, LOOK, PACK], BF16, f"x1_bf{b}") for b in range(2)]
+        x2_bf = [sbuf([P, LOOK, PACK], BF16, f"x2_bf{b}") for b in range(2)]
+        bias = sbuf([P, 8], F32, "bias")
+
+        def put(s):
+            factor = wd_nat if s < 4 else wd_dealt[s - 4]
+            pieces = 2 if s == 0 else 1
+            width = S // pieces
+            for h in range(pieces):
+                cols = slice(width * h, width * (h + 1))
+                nc.vector.tensor_tensor(
+                    pages[s][:].indirect(place[:, width // 16 * h : width // 16 * (h + 1)]), sums[s][:, cols], factor[:, cols], ALU.mult
+                )
+
+        def times_gain(b, t, cols):
+            nc.scalar.activation(out=x2_bf[b][:, cols, t], in_=opened[b][:, t, cols], func=ACT.Copy, scale=gain_sb[:, b, t : t + 1])
+
+        def open_rows(s):
+            b, t = divmod(s, PACK)
+            top = sbuf([P, 1], F32, f"top{s}", tag="top", bufs=2)
+            nc.vector.reduce_max(top[:], pages[s][:], AXIS.X)
+            nc.scalar.activation(out=bias[:, s : s + 1], in_=top[:], func=ACT.Copy, scale=slope[b][:, t : t + 1])
+            if b == 0:
+                fetched = sbuf([P, LOOK], F32, f"fetched{s}", tag="small", bufs=4)
+                dst = fetched[:]
+            else:
+                dst = opened[b][:, t, :]
+            nc.scalar.activation(
+                out=dst, in_=pages[s][:].indirect(look[:]), func=ACT.Sigmoid, bias=bias[:, s : s + 1], scale=steep_sb[b][:, t : t + 1]
+            )
+            if b == 0:
+                for i in range(PACK):
+                    nc.gpsimd.dma_start(out=opened[0][32 * s : 32 * (s + 1), i, :], in_=fetched[i:P:PACK, :])
+
+        def times_wear(b, cols):
+            nc.vector.tensor_tensor(
+                x1_bf[b][:, cols, :].rearrange("p (c i) t -> p c t i", i=4),
+                opened[b][:, :, cols].rearrange("p t (c i) -> p c t i", i=4),
+                wear_sb[b][:, :, cols].rearrange("p t (c i) -> p c t i", i=4),
+                ALU.mult,
+            )
+
+        x_codes = {(w, b): sbuf([P, LOOK], U32, f"x{w}_codes{b}") for w in range(2) for b in range(2)}
+        x_sc = {(w, b): sbuf([P, LOOK], U8, f"x{w}_sc{b}") for w in range(2) for b in range(2)}
+
+        def quantise_x(w, b, cols):
+            grouped = (x1_bf, x2_bf)[w][b]
+            nc.vector.quantize_mx(
+                out=x_codes[w, b][:, cols].bitcast(FP8X4), scales=x_sc[w, b][:, cols], in_=grouped[:, cols, :].rearrange("p m t -> p (m t)")
+            )
+
+        y_ps = [psum.tile([P, PACK, QUARTER], F32, name=f"y_ps{q}") for q in range(4)]
+        w5_q = []
+        w4_w = sbuf([P, 2, 2 * N], U8, "w4_w")
+        w4_sc = sbuf([P, 2, N], U8, "w4_sc")
+
+        def second_product(b, q):
+            cols = slice(QUARTER * q, QUARTER * (q + 1))
+            for w in range(2):
+                for t in range(PACK):
+                    if w == 0:
+                        codes = w4_w[:, b, 2 * P * t : 2 * P * (t + 1)].bitcast(FP4X4)
+                        scales = w4_sc[:, b, P * t : P * (t + 1)]
+                    else:
+                        codes = w5_q[b][0][:, P * t : P * (t + 1)].bitcast(FP8X4)
+                        scales = w5_q[b][1][:, P * t : P * (t + 1)]
+                    nc.tensor.matmul_mx(
+                        out=y_ps[q][:, t, :], lhsT=codes, lhsT_scale=scales,
+                        rhs=x_codes[w, b][:, cols].bitcast(FP8X4), rhs_scale=x_sc[w, b][:, cols],
+                        start=(b == 0 and w == 0 and t == 0), stop=(b == 1 and w == 1 and t == PACK - 1),
+                    )
+
+        everything = slice(0, LOOK)
+        for s in range(8):
+            put(s)
+            if s == 1:
+                for a in range(2):
+                    codes, scales = quantise_dealt(w1_raw[a], f"w1_dealt{a}")
+                    for t in range(PACK):
+                        w1_codes[4 + t, a] = codes[:, P * t : P * (t + 1)]
+                        w1_sc[4 + t, a] = scales[:, P * t : P * (t + 1)]
+                load_second_stage(1)
+            if s in (2, 3):
+                w5_q.append(quantise_dealt(w5_raw[s - 2], f"w5_{s - 2}"))
+            if s == 4:
+                nc.scalar.copy(
+                    out=w4_w[:].bitcast(U16).rearrange("p a (t m) -> p a t m", t=PACK),
+                    in_=w4_raw[:].bitcast(U16).rearrange("p a (m t) -> p a t m", t=PACK),
+                )
+                nc.vector.tensor_copy(
+                    out=w4_sc[:].rearrange("p a (t m) -> p a t m", t=PACK), in_=w4_sc_raw[:].rearrange("p a (m t) -> p a t m", t=PACK)
+                )
+            if s + 2 < 8:
+                first_product(s + 2)
+            open_rows(s)
+            if s + 6 < 8:
+                load_page(s + 6)
+            if 4 <= s < 7:
+                times_gain(1, s - 4, everything)
+            if s == 4:
+                for t in range(PACK):
+                    times_gain(0, t, everything)
+                times_wear(0, everything)
+            if s == 5:
+                quantise_x(0, 0, everything)
+                quantise_x(1, 0, everything)
+                for q in range(4):
+                    second_product(0, q)
+
+        y_codes = sbuf([P, LOOK], U32, "y_codes")
+        y_sc = sbuf([P, LOOK], U8, "y_sc")
+        out_rows = out_0.rearrange("(p t) m -> p t m", t=PACK)
+        out_words = out_1[0].rearrange("p m t -> p (m t)").bitcast(I32)
+        quarters = [slice(QUARTER * q, QUARTER * (q + 1)) for q in range(4)]
+        for cols in quarters:
+            times_gain(1, PACK - 1, cols)
+        y_bf = {}
+
+        def close(q):
+            cols = quarters[q]
+            y = sbuf([P, PACK, QUARTER], F32, f"y{q}", tag="small", bufs=4)
+            nc.scalar.copy(out=y[:], in_=y_ps[q][:])
+            nc.sync.dma_start(out=out_rows[:, :, cols], in_=y[:])
+            y_bf[q] = sbuf([P, QUARTER, PACK], BF16, f"y_bf{q}")
+            nc.vector.tensor_copy(out=y_bf[q][:].rearrange("p (c i) t -> p c t i", i=4), in_=y[:].rearrange("p t (c i) -> p c t i", i=4))
+
+        def planes(q):
+            cols = quarters[q]
+            nc.vector.quantize_mx(out=y_codes[:, cols].bitcast(FP8X4), scales=y_sc[:, cols], in_=y_bf[q][:].rearrange("p m t -> p (m t)"))
+            nc.sync.dma_start(out=out_words[:, cols], in_=y_codes[:, cols].bitcast(I32))
+
+        times_wear(1, quarters[0])
+        for q in range(4):
+            if q + 1 < 4:
+                times_wear(1, quarters[q + 1])
+            quantise_x(0, 1, quarters[q])
+            quantise_x(1, 1, quarters[q])
+            second_product(1, q)
+        for q in range(4):
+            close(q)
+            if q > 0:
+                planes(q - 1)
+        planes(3)
+        for q in range(4):
+            nc.scalar.dma_start(out=out_2[0, 4 * q : 4 * q + 4, :].bitcast(I32), in_=y_sc[32 * q : 32 * q + 4, :].bitcast(I32))

@@ -44,9 +44,9 @@ def tile_list_jetbridge_fault_scores_kernel(
         nc.sync.dma_start(pick[:], offs)
 
         tab_sc = sbuf([P, T], U8, "tab_sc")
-        nc.vector.memset(tab_sc[:].bitcast(I32), 0)
+        nc.gpsimd.memset(tab_sc[:].bitcast(I32), 0)
         for q in range(4):
-            nc.sync.dma_start(out=tab_sc[32 * q : 32 * q + 8, :].bitcast(I32), in_=tab_scales[:, 4 * q : 4 * q + 4, :].bitcast(I32))
+            nc.scalar.dma_start(out=tab_sc[32 * q : 32 * q + 8, :].bitcast(I32), in_=tab_scales[:, 4 * q : 4 * q + 4, :].bitcast(I32))
         tab_w = [sbuf([P, T], I32, f"tab_w{a}") for a in range(2)]
 
         def load_tab(a):
@@ -60,7 +60,7 @@ def tile_list_jetbridge_fault_scores_kernel(
 
         def load_w1_nat(u):
             for a in range(2):
-                w1_nat[u, a] = sbuf([P, PACK, 256], F32, f"w1_nat{u}{a}", tag="raw4", bufs=4)
+                w1_nat[u, a] = sbuf([P, PACK, 256], F32, f"w1_nat{u}{a}", tag=f"raw4_{2 * u + a}")
                 nc.sync.dma_start(out=w1_nat[u, a][:], in_=k_rows(w1, a, 256 * u, 256 * (u + 1)))
 
         load_w1_nat(0)
@@ -102,7 +102,7 @@ def tile_list_jetbridge_fault_scores_kernel(
             grouped = sbuf([P, 2, P, PACK], BF16, f"w1_bf{s}", tag="w1_bf", bufs=2)
             for a in range(2):
                 raw = w1_nat[s // 2, a][:, :, P * (s % 2) : P * (s % 2 + 1)]
-                nc.scalar.copy(out=grouped[:, a].rearrange("p (c i) j -> p c j i", i=4), in_=raw.rearrange("p j (c i) -> p c j i", i=4))
+                nc.scalar.copy(out=grouped[:, a].rearrange("p (c i) j -> p c j i", i=2), in_=raw.rearrange("p j (c i) -> p c j i", i=2))
             codes = sbuf([P, 2 * P], U32, f"w1_codes{s}")
             scales = sbuf([P, 2 * P], U8, f"w1_sc{s}")
             nc.vector.quantize_mx(out=codes[:].bitcast(FP8X4), scales=scales[:], in_=grouped[:].rearrange("p a c j -> p (a c j)"))
@@ -110,12 +110,14 @@ def tile_list_jetbridge_fault_scores_kernel(
                 w1_codes[s, a] = codes[:, P * a : P * (a + 1)]
                 w1_sc[s, a] = scales[:, P * a : P * (a + 1)]
 
-        def quantise_dealt(raw, name):
+        def round_dealt(raw, name):
             grouped = sbuf([P, PACK, P, PACK], BF16, name + "_bf", tag="dealt_bf", bufs=2)
             nc.scalar.copy(out=grouped[:].rearrange("p t m j -> p m j t"), in_=raw[:].rearrange("p j (m t) -> p m j t", t=PACK))
-            codes = sbuf([P, PASS], U32, name + "_codes")
+            return grouped
+
+        def quantise_dealt(grouped, codes, name):
             scales = sbuf([P, PASS], U8, name + "_sc")
-            nc.vector.quantize_mx(out=codes[:].bitcast(FP8X4), scales=scales[:], in_=grouped[:].rearrange("p t m j -> p (t m j)"))
+            nc.vector.quantize_mx(out=codes.bitcast(FP8X4), scales=scales[:], in_=grouped[:].rearrange("p t m j -> p (t m j)"))
             return codes, scales
 
         quantise_w1_nat(0)
@@ -173,7 +175,7 @@ def tile_list_jetbridge_fault_scores_kernel(
 
         wd_dealt = []
         for t in range(PACK):
-            dealt = sbuf([P, S], F32, f"wd_dealt{t}", tag="raw4", bufs=4)
+            dealt = sbuf([P, S], F32, f"wd_dealt{t}", tag=f"raw4_{t}")
             for g in range(4):
                 nc.sync.dma_start(out=dealt[32 * g : 32 * (g + 1), :], in_=wd_nat[t:P:PACK, :])
             wd_dealt.append(dealt)
@@ -245,13 +247,13 @@ def tile_list_jetbridge_fault_scores_kernel(
 
         def times_wear(b, cols):
             nc.vector.tensor_tensor(
-                x1_bf[b][:, cols, :].rearrange("p (c i) t -> p c t i", i=4),
-                opened[b][:, :, cols].rearrange("p t (c i) -> p c t i", i=4),
-                wear_sb[b][:, :, cols].rearrange("p t (c i) -> p c t i", i=4),
+                x1_bf[b][:, cols, :].rearrange("p (c i) t -> p c t i", i=2),
+                opened[b][:, :, cols].rearrange("p t (c i) -> p c t i", i=2),
+                wear_sb[b][:, :, cols].rearrange("p t (c i) -> p c t i", i=2),
                 ALU.mult,
             )
 
-        x_codes = {(w, b): sbuf([P, LOOK], U32, f"x{w}_codes{b}") for w in range(2) for b in range(2)}
+        x_codes = {(w, 1): sbuf([P, LOOK], U32, f"x{w}_codes1") for w in range(2)}
         x_sc = {(w, b): sbuf([P, LOOK], U8, f"x{w}_sc{b}") for w in range(2) for b in range(2)}
 
         def quantise_x(w, b, cols):
@@ -265,9 +267,9 @@ def tile_list_jetbridge_fault_scores_kernel(
         w4_w = sbuf([P, 2, 2 * N], U8, "w4_w")
         w4_sc = sbuf([P, 2, N], U8, "w4_sc")
 
-        def second_product(b, q):
+        def second_product(b, q, which):
             cols = slice(QUARTER * q, QUARTER * (q + 1))
-            for w in range(2):
+            for w in which:
                 for t in range(PACK):
                     if w == 0:
                         codes = w4_w[:, b, 2 * P * t : 2 * P * (t + 1)].bitcast(FP4X4)
@@ -286,13 +288,22 @@ def tile_list_jetbridge_fault_scores_kernel(
             put(s)
             if s == 1:
                 for a in range(2):
-                    codes, scales = quantise_dealt(w1_raw[a], f"w1_dealt{a}")
+                    name = f"w1_dealt{a}"
+                    codes, scales = quantise_dealt(round_dealt(w1_raw[a], name), sbuf([P, PASS], U32, name + "_codes")[:], name)
                     for t in range(PACK):
                         w1_codes[4 + t, a] = codes[:, P * t : P * (t + 1)]
                         w1_sc[4 + t, a] = scales[:, P * t : P * (t + 1)]
                 load_second_stage(1)
-            if s in (2, 3):
-                w5_q.append(quantise_dealt(w5_raw[s - 2], f"w5_{s - 2}"))
+            if s == 2:
+                w5_q.append(quantise_dealt(round_dealt(w5_raw[0], "w5_0"), sbuf([P, PASS], U32, "w5_0_codes")[:], "w5_0"))
+            if s == 3:
+                w5_last = round_dealt(w5_raw[1], "w5_1")
+            if s == 7:
+                late = sbuf([P, 3, LOOK], U32, "late_codes", tag="raw4_3")
+                x_codes[0, 0], x_codes[1, 0] = late[:, 0], late[:, 1]
+                quantise_x(0, 0, everything)
+                for q in range(4):
+                    second_product(0, q, [0])
             if s == 4:
                 nc.scalar.copy(
                     out=w4_w[:].bitcast(U16).rearrange("p a (t m) -> p a t m", t=PACK),
@@ -312,11 +323,11 @@ def tile_list_jetbridge_fault_scores_kernel(
                 for t in range(PACK):
                     times_gain(0, t, everything)
                 times_wear(0, everything)
-            if s == 5:
-                quantise_x(0, 0, everything)
+            if s == 7:
                 quantise_x(1, 0, everything)
                 for q in range(4):
-                    second_product(0, q)
+                    second_product(0, q, [1])
+                w5_q.append(quantise_dealt(w5_last, late[:, 2], "w5_1"))
 
         y_codes = sbuf([P, LOOK], U32, "y_codes")
         y_sc = sbuf([P, LOOK], U8, "y_sc")
@@ -333,7 +344,7 @@ def tile_list_jetbridge_fault_scores_kernel(
             nc.scalar.copy(out=y[:], in_=y_ps[q][:])
             nc.sync.dma_start(out=out_rows[:, :, cols], in_=y[:])
             y_bf[q] = sbuf([P, QUARTER, PACK], BF16, f"y_bf{q}")
-            nc.vector.tensor_copy(out=y_bf[q][:].rearrange("p (c i) t -> p c t i", i=4), in_=y[:].rearrange("p t (c i) -> p c t i", i=4))
+            nc.vector.tensor_copy(out=y_bf[q][:].rearrange("p (c i) t -> p c t i", i=2), in_=y[:].rearrange("p t (c i) -> p c t i", i=2))
 
         def planes(q):
             cols = quarters[q]
@@ -346,11 +357,11 @@ def tile_list_jetbridge_fault_scores_kernel(
                 times_wear(1, quarters[q + 1])
             quantise_x(0, 1, quarters[q])
             quantise_x(1, 1, quarters[q])
-            second_product(1, q)
+            second_product(1, q, [0, 1])
         for q in range(4):
             close(q)
             if q > 0:
                 planes(q - 1)
         planes(3)
         for q in range(4):
-            nc.scalar.dma_start(out=out_2[0, 4 * q : 4 * q + 4, :].bitcast(I32), in_=y_sc[32 * q : 32 * q + 4, :].bitcast(I32))
+            (nc.scalar, nc.sync)[q % 2].dma_start(out=out_2[0, 4 * q : 4 * q + 4, :].bitcast(I32), in_=y_sc[32 * q : 32 * q + 4, :].bitcast(I32))

from contextlib import ExitStack

import concourse.mybir as mybir
from concourse.masks import make_identity

K, H, N, T, S, T2, LOOK = 1024, 1024, 512, 2048, 1024, 2048, 512
FLOPS = 2 * K * H * S + 2 * 2 * H * N * LOOK

F32 = mybir.dt.float32
BF16 = mybir.dt.bfloat16
I32 = mybir.dt.int32
U32 = mybir.dt.uint32
U16 = mybir.dt.uint16
U8 = mybir.dt.uint8
FP8X4 = mybir.dt.float8_e4m3fn_x4
FP4X4 = mybir.dt.float4_e2m1fn_x4
ALU = mybir.AluOpType
ACT = mybir.ActivationFunctionType
AXIS = mybir.AxisListType

P = 128
PACK = 4
PASS = P * PACK
BANK = 512
QUARTER = 128


def tile_list_jetbridge_fault_scores_kernel(
    tc, tab_words, tab_scales, offs, offs2, offs3, w1, duty, wgs, page0, steep, share, wear, gain,
    w4_words, w4_scales, w5, out_0, out_1, out_2,
):
    nc = tc.nc
    with ExitStack() as ctx:
        lists = ctx.enter_context(tc.tile_pool(name="lists", bufs=1))
        sb = ctx.enter_context(tc.tile_pool(name="sb", bufs=1))
        psum = ctx.enter_context(tc.psum_pool(name="psum", bufs=1))

        def sbuf(shape, dtype, name, tag=None, bufs=1):
            return sb.tile(shape, dtype, name=name, tag=tag or name, bufs=bufs, align_bytes=64)

        pick = lists.tile([P, S // 16], U16, name="pick")
        place = lists.tile([P, S // 16], U16, name="place")
        look = lists.tile([P, LOOK // 16], U16, name="look")
        nc.sync.dma_start(pick[:], offs)

        tab_sc = sbuf([P, T], U8, "tab_sc")
        nc.gpsimd.memset(tab_sc[:].bitcast(I32), 0)
        for q in range(4):
            nc.scalar.dma_start(out=tab_sc[32 * q : 32 * q + 8, :].bitcast(I32), in_=tab_scales[:, 4 * q : 4 * q + 4, :].bitcast(I32))
        tab_w = [sbuf([P, T], I32, f"tab_w{a}") for a in range(2)]

        def load_tab(a):
            nc.sync.dma_start(out=tab_w[a][:], in_=tab_words[a].rearrange("p t i -> p (t i)").bitcast(I32))

        def k_rows(w, a, c0, c1):
            return w[PASS * a : PASS * (a + 1), c0:c1].rearrange("(p j) c -> p j c", j=PACK)

        load_tab(0)
        w1_nat = {}

        def load_w1_nat(u):
            for a in range(2):
                w1_nat[u, a] = sbuf([P, PACK, 256], F32, f"w1_nat{u}{a}", tag=f"raw4_{2 * u + a}")
                nc.sync.dma_start(out=w1_nat[u, a][:], in_=k_rows(w1, a, 256 * u, 256 * (u + 1)))

        load_w1_nat(0)
        load_tab(1)
        duty_col = sbuf([P, 2, PACK], F32, "duty_col")
        nc.sync.dma_start(out=duty_col[:], in_=duty.rearrange("(h p c) -> p h c", h=2, c=PACK))
        wd_nat = sbuf([P, S], F32, "wd_nat")
        nc.sync.dma_start(out=wd_nat[:], in_=wgs)
        nc.sync.dma_start(place[:], offs2)

        pages = {}

        def load_page(s):
            pages[s] = sbuf([P, T2], F32, f"page{s}", tag="page", bufs=6)
            if s < 4:
                rows = page0[P * s : P * (s + 1), :]
            else:
                rows = page0[PASS:, :].rearrange("(p t) c -> p t c", t=PACK)[:, s - 4, :]
            nc.sync.dma_start(out=pages[s][:], in_=rows)

        load_page(0)
        load_w1_nat(1)

        got_sc = sbuf([P, S], U8, "got_sc")
        nc.vector.tensor_copy(got_sc[:], tab_sc[:].indirect(pick[:]))
        got_w = {}

        def gather_words(a):
            for h in range(2):
                got_w[a, h] = sbuf([P, BANK], U32, f"got_w{a}{h}")
                nc.vector.tensor_copy(got_w[a, h][:], tab_w[a][:].bitcast(U32).indirect(pick[:, 32 * h : 32 * (h + 1)]))

        gather_words(0)

        w1_codes = {}
        w1_sc = {}

        def quantise_w1_nat(s):
            grouped = sbuf([P, 2, P, PACK], BF16, f"w1_bf{s}", tag="w1_bf", bufs=2)
            for a in range(2):
                raw = w1_nat[s // 2, a][:, :, P * (s % 2) : P * (s % 2 + 1)]
                nc.scalar.copy(out=grouped[:, a].rearrange("p (c i) j -> p c j i", i=2), in_=raw.rearrange("p j (c i) -> p c j i", i=2))
            codes = sbuf([P, 2 * P], U32, f"w1_codes{s}")
            scales = sbuf([P, 2 * P], U8, f"w1_sc{s}")
            nc.vector.quantize_mx(out=codes[:].bitcast(FP8X4), scales=scales[:], in_=grouped[:].rearrange("p a c j -> p (a c j)"))
            for a in range(2):
                w1_codes[s, a] = codes[:, P * a : P * (a + 1)]
                w1_sc[s, a] = scales[:, P * a : P * (a + 1)]

        def round_dealt(raw, name):
            grouped = sbuf([P, PACK, P, PACK], BF16, name + "_bf", tag="dealt_bf", bufs=2)
            nc.scalar.copy(out=grouped[:].rearrange("p t m j -> p m j t"), in_=raw[:].rearrange("p j (m t) -> p m j t", t=PACK))
            return grouped

        def quantise_dealt(grouped, codes, name):
            scales = sbuf([P, PASS], U8, name + "_sc")
            nc.vector.quantize_mx(out=codes.bitcast(FP8X4), scales=scales[:], in_=grouped[:].rearrange("p t m j -> p (t m j)"))
            return codes, scales

        quantise_w1_nat(0)
        gather_words(1)

        ident = sbuf([P, P], F32, "ident")
        make_identity(nc, ident[:])
        for h in range(2):
            spread = psum.tile([P, PACK, P], F32, name=f"duty_ps{h}", tag="h", bufs=4)
            for c in range(PACK):
                nc.tensor.transpose(spread[:, c, :], duty_col[:, h, c : c + 1].to_broadcast([P, P]), ident[:])
            cols = wd_nat[:, BANK * h : BANK * (h + 1)].rearrange("p (n c) -> p n c", c=PACK)
            nc.vector.tensor_tensor(cols, spread[:].rearrange("p c n -> p n c"), cols, ALU.mult)

        quantise_w1_nat(1)

        sums = {}

        def first_product(s):
            sums[s] = sbuf([P, S], F32, f"sums{s}", tag="sums", bufs=3)
            for h in range(2):
                bank = psum.tile([P, BANK], F32, name=f"h_ps{s}{h}", tag="h", bufs=4)
                for a in range(2):
                    nc.tensor.matmul_mx(
                        out=bank[:], lhsT=w1_codes[s, a].bitcast(FP8X4), lhsT_scale=w1_sc[s, a],
                        rhs=got_w[a, h][:].bitcast(FP8X4), rhs_scale=got_sc[4 * a :, BANK * h : BANK * (h + 1)],
                        start=(a == 0), stop=(a == 1),
                    )
                nc.scalar.copy(out=sums[s][:, BANK * h : BANK * (h + 1)], in_=bank[:])

        first_product(0)
        first_product(1)

        nc.sync.dma_start(look[:], offs3)
        steep_sb, share_sb = [], []
        for name, vec, dst in (("steep", steep, steep_sb), ("share", share, share_sb)):
            nat = sbuf([P, PACK], F32, name + "_nat")
            with nc.allow_non_contiguous_dma(reason="one value of a row vector for each partition"):
                nc.sync.dma_start(out=nat[:], in_=vec[:PASS].rearrange("(s p) -> p s", p=P))
            dealt = sbuf([P, PACK], F32, name + "_dealt")
            nc.sync.dma_start(out=dealt[:], in_=vec[PASS:].rearrange("(p t) -> p t", t=PACK))
            dst.extend([nat, dealt])
        gain_sb = sbuf([P, 2, PACK], F32, "gain_sb")
        nc.sync.dma_start(out=gain_sb[:], in_=gain.rearrange("(b p t) -> p b t", b=2, t=PACK))
        load_page(1)
        w1_raw = []
        for a in range(2):
            raw = sbuf([P, PACK, PASS], F32, f"w1_raw{a}", tag="raw8", bufs=4)
            nc.sync.dma_start(out=raw[:], in_=k_rows(w1, a, PASS, H))
            w1_raw.append(raw)
        load_page(2)

        quantise_w1_nat(2)
        quantise_w1_nat(3)

        wd_dealt = []
        for t in range(PACK):
            dealt = sbuf([P, S], F32, f"wd_dealt{t}", tag=f"raw4_{t}")
            for g in range(4):
                nc.sync.dma_start(out=dealt[32 * g : 32 * (g + 1), :], in_=wd_nat[t:P:PACK, :])
            wd_dealt.append(dealt)
        load_page(3)

        w5_raw, wear_sb = [], []

        def load_second_stage(b):
            raw = sbuf([P, PACK, N], F32, f"w5_raw{b}", tag="raw8", bufs=4)
            nc.sync.dma_start(out=raw[:], in_=k_rows(w5, b, 0, N))
            w5_raw.append(raw)
            rows = sbuf([P, PACK, LOOK], F32, f"wear{b}", tag="raw8", bufs=4)
            nc.sync.dma_start(out=rows[:], in_=k_rows(wear, b, 0, LOOK))
            wear_sb.append(rows)

        load_second_stage(0)
        load_page(4)
        load_page(5)
        w4_raw = sbuf([P, 2, 2 * N], U8, "w4_raw")
        nc.sync.dma_start(out=w4_raw[:].bitcast(I32), in_=w4_words.rearrange("a p c -> p a c").bitcast(I32))
        w4_sc_raw = sbuf([P, 2, N], U8, "w4_sc_raw")
        nc.gpsimd.memset(w4_sc_raw[:].bitcast(I32), 0)
        for q in range(4):
            nc.sync.dma_start(
                out=w4_sc_raw[32 * q : 32 * q + 4].bitcast(I32),
                in_=w4_scales[:, 4 * q : 4 * q + 4, :].rearrange("a r c -> r a c").bitcast(I32),
            )

        slope = []
        for b in range(2):
            neg = sbuf([P, PACK], F32, f"slope{b}")
            nc.vector.scalar_tensor_tensor(neg[:], steep_sb[b][:], -1.0, share_sb[b][:], ALU.mult, ALU.mult)
            slope.append(neg)

        opened = [sbuf([P, PACK, LOOK], F32, f"opened{b}") for b in range(2)]
        x1_bf = [sbuf([P, LOOK, PACK], BF16, f"x1_bf{b}") for b in range(2)]
        x2_bf = [sbuf([P, LOOK, PACK], BF16, f"x2_bf{b}") for b in range(2)]
        bias = sbuf([P, 8], F32, "bias")

        def put(s):
            factor = wd_nat if s < 4 else wd_dealt[s - 4]
            pieces = 2 if s == 0 else 1
            width = S // pieces
            for h in range(pieces):
                cols = slice(width * h, width * (h + 1))
                nc.vector.tensor_tensor(
                    pages[s][:].indirect(place[:, width // 16 * h : width // 16 * (h + 1)]), sums[s][:, cols], factor[:, cols], ALU.mult
                )

        def times_gain(b, t, cols):
            nc.scalar.activation(out=x2_bf[b][:, cols, t], in_=opened[b][:, t, cols], func=ACT.Copy, scale=gain_sb[:, b, t : t + 1])

        def open_rows(s):
            b, t = divmod(s, PACK)
            top = sbuf([P, 1], F32, f"top{s}", tag="top", bufs=2)
            nc.vector.reduce_max(top[:], pages[s][:], AXIS.X)
            nc.scalar.activation(out=bias[:, s : s + 1], in_=top[:], func=ACT.Copy, scale=slope[b][:, t : t + 1])
            if b == 0:
                fetched = sbuf([P, LOOK], F32, f"fetched{s}", tag="small", bufs=4)
                dst = fetched[:]
            else:
                dst = opened[b][:, t, :]
            nc.scalar.activation(
                out=dst, in_=pages[s][:].indirect(look[:]), func=ACT.Sigmoid, bias=bias[:, s : s + 1], scale=steep_sb[b][:, t : t + 1]
            )
            if b == 0:
                for i in range(PACK):
                    nc.gpsimd.dma_start(out=opened[0][32 * s : 32 * (s + 1), i, :], in_=fetched[i:P:PACK, :])

        def times_wear(b, cols):
            nc.vector.tensor_tensor(
                x1_bf[b][:, cols, :].rearrange("p (c i) t -> p c t i", i=2),
                opened[b][:, :, cols].rearrange("p t (c i) -> p c t i", i=2),
                wear_sb[b][:, :, cols].rearrange("p t (c i) -> p c t i", i=2),
                ALU.mult,
            )

        x_codes = {(w, 1): sbuf([P, LOOK], U32, f"x{w}_codes1") for w in range(2)}
        x_sc = {(w, b): sbuf([P, LOOK], U8, f"x{w}_sc{b}") for w in range(2) for b in range(2)}

        def quantise_x(w, b, cols):
            grouped = (x1_bf, x2_bf)[w][b]
            nc.vector.quantize_mx(
                out=x_codes[w, b][:, cols].bitcast(FP8X4), scales=x_sc[w, b][:, cols], in_=grouped[:, cols, :].rearrange("p m t -> p (m t)")
            )

        y_ps = [psum.tile([P, PACK, QUARTER], F32, name=f"y_ps{q}") for q in range(4)]
        w5_q = []
        w4_w = sbuf([P, 2, 2 * N], U8, "w4_w")
        w4_sc = sbuf([P, 2, N], U8, "w4_sc")

        def second_product(b, q, which):
            cols = slice(QUARTER * q, QUARTER * (q + 1))
            for w in which:
                for t in range(PACK):
                    if w == 0:
                        codes = w4_w[:, b, 2 * P * t : 2 * P * (t + 1)].bitcast(FP4X4)
                        scales = w4_sc[:, b, P * t : P * (t + 1)]
                    else:
                        codes = w5_q[b][0][:, P * t : P * (t + 1)].bitcast(FP8X4)
                        scales = w5_q[b][1][:, P * t : P * (t + 1)]
                    nc.tensor.matmul_mx(
                        out=y_ps[q][:, t, :], lhsT=codes, lhsT_scale=scales,
                        rhs=x_codes[w, b][:, cols].bitcast(FP8X4), rhs_scale=x_sc[w, b][:, cols],
                        start=(b == 0 and w == 0 and t == 0), stop=(b == 1 and w == 1 and t == PACK - 1),
                    )

        everything = slice(0, LOOK)
        for s in range(8):
            put(s)
            if s == 1:
                for a in range(2):
                    name = f"w1_dealt{a}"
                    codes, scales = quantise_dealt(round_dealt(w1_raw[a], name), sbuf([P, PASS], U32, name + "_codes")[:], name)
                    for t in range(PACK):
                        w1_codes[4 + t, a] = codes[:, P * t : P * (t + 1)]
                        w1_sc[4 + t, a] = scales[:, P * t : P * (t + 1)]
                load_second_stage(1)
            if s == 2:
                w5_q.append(quantise_dealt(round_dealt(w5_raw[0], "w5_0"), sbuf([P, PASS], U32, "w5_0_codes")[:], "w5_0"))
            if s == 3:
                w5_last = round_dealt(w5_raw[1], "w5_1")
            if s == 7:
                late = sbuf([P, 3, LOOK], U32, "late_codes", tag="raw4_3")
                x_codes[0, 0], x_codes[1, 0] = late[:, 0], late[:, 1]
                quantise_x(0, 0, everything)
                for q in range(4):
                    second_product(0, q, [0])
            if s == 4:
                nc.scalar.copy(
                    out=w4_w[:].bitcast(U16).rearrange("p a (t m) -> p a t m", t=PACK),
                    in_=w4_raw[:].bitcast(U16).rearrange("p a (m t) -> p a t m", t=PACK),
                )
                nc.vector.tensor_copy(
                    out=w4_sc[:].rearrange("p a (t m) -> p a t m", t=PACK), in_=w4_sc_raw[:].rearrange("p a (m t) -> p a t m", t=PACK)
                )
            if s + 2 < 8:
                first_product(s + 2)
            open_rows(s)
            if s + 6 < 8:
                load_page(s + 6)
            if 4 <= s < 7:
                times_gain(1, s - 4, everything)
            if s == 4:
                for t in range(PACK):
                    times_gain(0, t, everything)
                times_wear(0, everything)
            if s == 7:
                quantise_x(1, 0, everything)
                for q in range(4):
                    second_product(0, q, [1])
                w5_q.append(quantise_dealt(w5_last, late[:, 2], "w5_1"))

        y_codes = sbuf([P, LOOK], U32, "y_codes")
        y_sc = sbuf([P, LOOK], U8, "y_sc")
        out_rows = out_0.rearrange("(p t) m -> p t m", t=PACK)
        out_words = out_1[0].rearrange("p m t -> p (m t)").bitcast(I32)
        quarters = [slice(QUARTER * q, QUARTER * (q + 1)) for q in range(4)]
        for cols in quarters:
            times_gain(1, PACK - 1, cols)
        y_bf = {}

        def close(q):
            cols = quarters[q]
            y = sbuf([P, PACK, QUARTER], F32, f"y{q}", tag="small", bufs=4)
            nc.scalar.copy(out=y[:], in_=y_ps[q][:])
            nc.sync.dma_start(out=out_rows[:, :, cols], in_=y[:])
            y_bf[q] = sbuf([P, QUARTER, PACK], BF16, f"y_bf{q}")
            nc.vector.tensor_copy(out=y_bf[q][:].rearrange("p (c i) t -> p c t i", i=2), in_=y[:].rearrange("p t (c i) -> p c t i", i=2))

        def planes(q):
            cols = quarters[q]
            nc.vector.quantize_mx(out=y_codes[:, cols].bitcast(FP8X4), scales=y_sc[:, cols], in_=y_bf[q][:].rearrange("p m t -> p (m t)"))
            nc.sync.dma_start(out=out_words[:, cols], in_=y_codes[:, cols].bitcast(I32))

        times_wear(1, quarters[0])
        for q in range(4):
            if q + 1 < 4:
                times_wear(1, quarters[q + 1])
            quantise_x(0, 1, quarters[q])
            quantise_x(1, 1, quarters[q])
            second_product(1, q, [0, 1])
        for q in range(4):
            close(q)
            if q > 0:
                planes(q - 1)
        planes(3)
        for q in range(4):
            (nc.scalar, nc.sync)[q % 2].dma_start(out=out_2[0, 4 * q : 4 * q + 4, :].bitcast(I32), in_=y_sc[32 * q : 32 * q + 4, :].bitcast(I32))
